import numpy as np
import ml_dtypes


def mxq(x, axis, fmt="e4m3"):
    dtype, down = {"e4m3": (ml_dtypes.float8_e4m3fn, 7), "e5m2": (ml_dtypes.float8_e5m2, 14)}[fmt]
    v = np.moveaxis(np.asarray(x, np.float32).astype(ml_dtypes.bfloat16).astype(np.float64), axis, -1)
    blocks = v.reshape(v.shape[:-1] + (-1, 32))
    amax = np.abs(blocks).max(-1, keepdims=True)
    byte = np.maximum(np.where(amax > 0, np.frexp(amax)[1] - 1 + 127, 0) - down, 1)
    scale = np.exp2(byte - 127.0)
    codes = (blocks / scale).astype(np.float32).astype(dtype).astype(np.float64)
    return np.moveaxis((codes * scale).reshape(v.shape), -1, axis)


WIDE = False


def mx_kscale(k):
    if not WIDE:
        return np.ones(k)
    levels = np.array([10, -10, 5, -5, 0])
    if k % 512:
        return np.exp2(np.random.permutation(np.resize(levels, k // 32))).repeat(32)
    a = np.empty((k // 512, 16))
    for p in range(k // 512):
        a[p, :8] = np.random.permutation(np.resize(levels, 8))
        for g in range(8):
            far = levels[np.abs(levels - a[p, g]) >= 10]
            a[p, g + 8] = far[np.random.randint(len(far))]
    return np.exp2(a.ravel()).repeat(32)


def f64(x):
    return np.asarray(x).astype(np.float64)


def striped8(idx):
    return np.concatenate([v.reshape(-1, 16).T for v in idx]).astype(np.uint16)


def unstriped8(offs):
    return np.stack([offs[16 * g:16 * g + 16].T.reshape(-1) for g in range(8)]).astype(np.int64)


def silu(v):
    return v / (1.0 + np.exp(-np.maximum(v, -700.0)))


K, M, T, S = 1024, 512, 1024, 512


def setup_inputs():
    n = np.random.standard_normal
    s = mx_kscale(K)[:, None]
    return {
        "xT": (n((K, T)) * s).astype(np.float32),
        "w": (n((K, M)) / np.sqrt(K) / s).astype(np.float32),
        "wgt": np.repeat(np.random.uniform(0.5, 2.0, (8, S)), 16, axis=0).astype(np.float32),
        "b": (0.3 * n(512)).astype(np.float32),
        "wgo": np.repeat(np.random.uniform(0.5, 2.0, (8, S)), 16, axis=0).astype(np.float32),
        "offs": striped8(np.stack([np.random.permutation(T)[:S] for _ in range(8)])),
        "offs2": striped8(np.stack([np.random.permutation(T)[:S] for _ in range(8)])),
    }


def reference(xT, w, wgt, b, wgo, offs, offs2):
    idx = unstriped8(offs)
    group = np.arange(K) % 512 // 64
    xg = f64(wgt)[np.arange(K) // 4 % 128] * f64(xT)[np.arange(K)[:, None], idx[group]]
    xT_ = mxq(xg, 0, "e4m3")
    w_ = mxq(f64(w), 0, "e4m3")
    y = w_.T @ xT_
    place = unstriped8(offs2)[np.arange(M) % 128 // 16]
    out = np.zeros((M, T))
    out[np.arange(M)[:, None], place] = f64(wgo)[np.arange(M) % 128] * (silu(y + f64(b)[:, None]))
    return out

@@ -1,0 +1,194 @@
+from contextlib import ExitStack
+
+import concourse.mybir as mybir
+from concourse.masks import make_identity
+
+K, M, T, S = 1024, 512, 1024, 512
+FLOPS = 2 * K * M * S
+
+F32 = mybir.dt.float32
+BF16 = mybir.dt.bfloat16
+U32 = mybir.dt.uint32
+U16 = mybir.dt.uint16
+U8 = mybir.dt.uint8
+FP8X4 = mybir.dt.float8_e4m3fn_x4
+MULT = mybir.AluOpType.mult
+SILU = mybir.ActivationFunctionType.Silu
+
+P = 128
+PACK = 4
+PASSES = K // (P * PACK)
+MT = M // P
+HALVES = 2
+H = S // HALVES
+HC = H // 16
+
+
+def tile_list_hboth_silu_kernel(tc, xT, w, wgt, b, wgo, offs, offs2, out):
+    nc = tc.nc
+    x_hbm = xT.rearrange("(a p i) t -> a p i t", p=P, i=PACK)
+    w_hbm = w.rearrange("(a p i) n -> a p i n", p=P, i=PACK)
+
+    with ExitStack() as ctx:
+        lists = ctx.enter_context(tc.tile_pool(name="lists", bufs=1))
+        keep = ctx.enter_context(tc.tile_pool(name="keep", bufs=1))
+        psum = ctx.enter_context(tc.psum_pool(name="psum", bufs=1))
+
+        offs_sb = lists.tile([P, S // 16], U16, name="offs_sb")
+        offs2_sb = lists.tile([P, S // 16], U16, name="offs2_sb")
+
+        wgt_sb = [keep.tile([P, H], F32, name=f"wgt{h}") for h in range(HALVES)]
+        wgo_sb = keep.tile([P, S], F32, name="wgo_sb")
+        x_sb = [[keep.tile([P, T], F32, name=f"x{a}{i}") for i in range(PACK)] for a in range(PASSES)]
+        w_raw = [[keep.tile([P, PACK, P], F32, name=f"wr{m}{a}") for a in range(PASSES)] for m in range(2)]
+        w_raw23 = [keep.tile([P, PACK, 2 * P], F32, name=f"wr23{a}") for a in range(PASSES)]
+        picked = [[keep.tile([P, PACK, H], F32, name=f"g{a}{h}") for h in range(HALVES)] for a in range(PASSES)]
+        x_bf = [[keep.tile([P, H, PACK], BF16, align_bytes=64, name=f"xb{a}{h}") for h in range(HALVES)] for a in range(PASSES)]
+        x_codes = [[keep.tile([P, H], U32, align_bytes=64, name=f"xc{a}{h}") for h in range(HALVES)] for a in range(PASSES)]
+        x_scales = [[keep.tile([P, H], U8, align_bytes=64, name=f"xs{a}{h}") for h in range(HALVES)] for a in range(PASSES)]
+        w_bf = [keep.tile([P, PASSES * P, PACK], BF16, align_bytes=64, name=f"wb{m}") for m in range(MT)]
+        w_codes = [keep.tile([P, PASSES * P], U32, align_bytes=64, name=f"wc{m}") for m in range(MT)]
+        w_scales = [keep.tile([P, PASSES * P], U8, align_bytes=64, name=f"ws{m}") for m in range(MT)]
+        window = [keep.tile([P, T], F32, name=f"win{m}") for m in range(MT)]
+        act = [[keep.tile([P, H], F32, name=f"act{m}{h}") for h in range(HALVES)] for m in range(MT)]
+
+        ident = keep.tile([P, P], F32, name="ident")
+        b_rows = keep.tile([P, P], F32, name="b_rows")
+        b_cols = keep.tile([P, MT], F32, name="b_cols")
+        warm_in = keep.tile([P, 1], F32, name="warm_in")
+        warm_out = keep.tile([P, 1], F32, name="warm_out")
+
+        nc.vector.memset(warm_in[:], 0.0)
+        nc.vector.memset(b_rows[:], 0.0)
+        nc.sync.dma_start(offs_sb[:], offs)
+        nc.sync.dma_start(out=wgt_sb[0][:], in_=wgt[:, 0:H])
+        nc.sync.dma_start(out=x_sb[0][0][:], in_=x_hbm[0, :, 0, :])
+        nc.sync.dma_start(out=wgt_sb[1][:], in_=wgt[:, H:S])
+        nc.scalar.activation(warm_out[:], warm_in[:], SILU)
+        for a in range(PASSES):
+            for i in range(PACK):
+                if a + i > 0:
+                    nc.sync.dma_start(out=x_sb[a][i][:], in_=x_hbm[a, :, i, :])
+        for a in range(PASSES):
+            nc.sync.dma_start(out=w_raw[0][a][:], in_=w_hbm[a, :, :, 0:P])
+        nc.sync.dma_start(offs2_sb[:], offs2)
+        nc.sync.dma_start(out=wgo_sb[:], in_=wgo)
+        for a in range(PASSES):
+            nc.sync.dma_start(out=w_raw[1][a][:], in_=w_hbm[a, :, :, P : 2 * P])
+        for a in range(PASSES):
+            nc.sync.dma_start(out=w_raw23[a][:], in_=w_hbm[a, :, :, 2 * P : 4 * P])
+
+        for m in range(MT):
+            nc.vector.memset(window[m][:], 0.0)
+        make_identity(nc, ident[:])
+        nc.scalar.dma_start(out=b_rows[0:MT, :], in_=b.rearrange("(m p) -> m p", p=P))
+        b_ps = psum.tile([P, P], F32, name="b_ps")
+        nc.tensor.transpose(b_ps[:], b_rows[:], ident[:])
+        nc.scalar.copy(out=b_cols[:], in_=b_ps[:, 0:MT])
+
+        def gather(a, i, h):
+            nc.vector.tensor_tensor(
+                picked[a][h][:, i, :],
+                x_sb[a][i][:].indirect(offs_sb[:, h * HC : (h + 1) * HC]),
+                wgt_sb[h][:],
+                MULT,
+            )
+
+        def interleave_x(a, h):
+            nc.scalar.copy(
+                out=x_bf[a][h][:].rearrange("p (c e) i -> p c i e", e=4),
+                in_=picked[a][h][:].rearrange("p i (c e) -> p c i e", e=4),
+            )
+
+        def quantize_x(a, h):
+            nc.vector.quantize_mx(
+                out=x_codes[a][h][:].bitcast(FP8X4),
+                scales=x_scales[a][h][:],
+                in_=x_bf[a][h][:].rearrange("p c i -> p (c i)"),
+            )
+
+        def interleave_w(m, a, copy):
+            raw = w_raw[m][a][:] if m < 2 else w_raw23[a][:, :, (m - 2) * P : (m - 1) * P]
+            copy(
+                out=w_bf[m][:, a * P : (a + 1) * P, :].rearrange("p (c e) i -> p c i e", e=4),
+                in_=raw.rearrange("p i (c e) -> p c i e", e=4),
+            )
+
+        def quantize_w(m):
+            nc.vector.quantize_mx(
+                out=w_codes[m][:].bitcast(FP8X4),
+                scales=w_scales[m][:],
+                in_=w_bf[m][:].rearrange("p c i -> p (c i)"),
+            )
+
+        def product(m, h):
+            acc = psum.tile([P, H], F32, name="acc", bufs=6)
+            for a in range(PASSES):
+                nc.tensor.matmul_mx(
+                    out=acc[:],
+                    lhsT=w_codes[m][:, a * P : (a + 1) * P].bitcast(FP8X4),
+                    lhsT_scale=w_scales[m][:, a * P : (a + 1) * P],
+                    rhs=x_codes[a][h][:].bitcast(FP8X4),
+                    rhs_scale=x_scales[a][h][:],
+                    start=(a == 0),
+                    stop=(a == PASSES - 1),
+                )
+            nc.scalar.activation(act[m][h][:], acc[:], SILU, bias=b_cols[:, m : m + 1])
+
+        def scatter(m, h):
+            nc.vector.tensor_tensor(
+                window[m][:].indirect(offs2_sb[:, h * HC : (h + 1) * HC]),
+                act[m][h][:],
+                wgo_sb[:, h * H : (h + 1) * H],
+                MULT,
+            )
+
+        def store(m):
+            nc.sync.dma_start(out=out[m * P : (m + 1) * P, :], in_=window[m][:])
+
+        for i in range(PACK):
+            for h in range(HALVES):
+                gather(0, i, h)
+        for h in range(HALVES):
+            interleave_x(0, h)
+        for i in range(PACK):
+            for h in range(HALVES):
+                gather(1, i, h)
+            if i >= 2:
+                quantize_x(0, i - 2)
+        for h in range(HALVES):
+            interleave_x(1, h)
+        for a in range(PASSES):
+            interleave_w(0, a, nc.vector.tensor_copy)
+        quantize_x(1, 0)
+        quantize_w(0)
+        product(0, 0)
+        quantize_x(1, 1)
+        product(0, 1)
+        for a in range(PASSES):
+            interleave_w(1, a, nc.scalar.copy)
+        scatter(0, 0)
+        quantize_w(1)
+        product(1, 0)
+        for a in range(PASSES):
+            interleave_w(2, a, nc.scalar.copy)
+        scatter(0, 1)
+        store(0)
+        quantize_w(2)
+        product(2, 0)
+        product(1, 1)
+        scatter(1, 0)
+        for a in range(PASSES):
+            interleave_w(3, a, nc.scalar.copy)
+        scatter(2, 0)
+        quantize_w(3)
+        product(3, 0)
+        scatter(1, 1)
+        store(1)
+        product(2, 1)
+        scatter(3, 0)
+        product(3, 1)
+        scatter(2, 1)
+        store(2)
+        scatter(3, 1)
+        store(3)

@@ -40,8 +40,8 @@ def tile_list_hboth_silu_kernel(tc, xT, w, wgt, b, wgo, offs, offs2, out):
         wgt_sb = [keep.tile([P, H], F32, name=f"wgt{h}") for h in range(HALVES)]
         wgo_sb = keep.tile([P, S], F32, name="wgo_sb")
         x_sb = [[keep.tile([P, T], F32, name=f"x{a}{i}") for i in range(PACK)] for a in range(PASSES)]
-        w_raw = [[keep.tile([P, PACK, P], F32, name=f"wr{m}{a}") for a in range(PASSES)] for m in range(2)]
-        w_raw23 = [keep.tile([P, PACK, 2 * P], F32, name=f"wr23{a}") for a in range(PASSES)]
+        w_raw0 = keep.tile([P, PACK, M], F32, name="w_raw0")
+        w_raw1 = [keep.tile([P, PACK, 2 * P], F32, name=f"w_raw1{g}") for g in range(2)]
         picked = [[keep.tile([P, PACK, H], F32, name=f"g{a}{h}") for h in range(HALVES)] for a in range(PASSES)]
         x_bf = [[keep.tile([P, H, PACK], BF16, align_bytes=64, name=f"xb{a}{h}") for h in range(HALVES)] for a in range(PASSES)]
         x_codes = [[keep.tile([P, H], U32, align_bytes=64, name=f"xc{a}{h}") for h in range(HALVES)] for a in range(PASSES)]
@@ -61,26 +61,25 @@ def tile_list_hboth_silu_kernel(tc, xT, w, wgt, b, wgo, offs, offs2, out):
         nc.vector.memset(warm_in[:], 0.0)
         nc.vector.memset(b_rows[:], 0.0)
         nc.sync.dma_start(offs_sb[:], offs)
-        nc.sync.dma_start(out=wgt_sb[0][:], in_=wgt[:, 0:H])
         nc.sync.dma_start(out=x_sb[0][0][:], in_=x_hbm[0, :, 0, :])
+        nc.sync.dma_start(out=wgt_sb[0][:], in_=wgt[:, 0:H])
         nc.sync.dma_start(out=wgt_sb[1][:], in_=wgt[:, H:S])
         nc.scalar.activation(warm_out[:], warm_in[:], SILU)
-        for a in range(PASSES):
-            for i in range(PACK):
-                if a + i > 0:
-                    nc.sync.dma_start(out=x_sb[a][i][:], in_=x_hbm[a, :, i, :])
-        for a in range(PASSES):
-            nc.sync.dma_start(out=w_raw[0][a][:], in_=w_hbm[a, :, :, 0:P])
+        def load_x(a, i):
+            nc.sync.dma_start(out=x_sb[a][i][:], in_=x_hbm[a, :, i, :])
+
+        for a, i in ((0, 1), (0, 2), (0, 3), (1, 0), (1, 1), (1, 2)):
+            load_x(a, i)
+        nc.sync.dma_start(out=w_raw0[:], in_=w_hbm[0])
+        load_x(1, 3)
+        for g in range(2):
+            nc.sync.dma_start(out=w_raw1[g][:], in_=w_hbm[1, :, :, 2 * P * g : 2 * P * (g + 1)])
         nc.sync.dma_start(offs2_sb[:], offs2)
         nc.sync.dma_start(out=wgo_sb[:], in_=wgo)
-        for a in range(PASSES):
-            nc.sync.dma_start(out=w_raw[1][a][:], in_=w_hbm[a, :, :, P : 2 * P])
-        for a in range(PASSES):
-            nc.sync.dma_start(out=w_raw23[a][:], in_=w_hbm[a, :, :, 2 * P : 4 * P])
 
-        for m in range(MT):
-            nc.vector.memset(window[m][:], 0.0)
         make_identity(nc, ident[:])
+        for m in range(MT):
+            (nc.vector if m < 2 else nc.gpsimd).memset(window[m][:], 0.0)
         nc.scalar.dma_start(out=b_rows[0:MT, :], in_=b.rearrange("(m p) -> m p", p=P))
         b_ps = psum.tile([P, P], F32, name="b_ps")
         nc.tensor.transpose(b_ps[:], b_rows[:], ident[:])
@@ -108,7 +107,7 @@ def tile_list_hboth_silu_kernel(tc, xT, w, wgt, b, wgo, offs, offs2, out):
             )
 
         def interleave_w(m, a, copy):
-            raw = w_raw[m][a][:] if m < 2 else w_raw23[a][:, :, (m - 2) * P : (m - 1) * P]
+            raw = w_raw0[:, :, m * P : (m + 1) * P] if a == 0 else w_raw1[m // 2][:, :, (m % 2) * P : (m % 2 + 1) * P]
             copy(
                 out=w_bf[m][:, a * P : (a + 1) * P, :].rearrange("p (c e) i -> p c i e", e=4),
                 in_=raw.rearrange("p i (c e) -> p c i e", e=4),
@@ -122,7 +121,7 @@ def tile_list_hboth_silu_kernel(tc, xT, w, wgt, b, wgo, offs, offs2, out):
             )
 
         def product(m, h):
-            acc = psum.tile([P, H], F32, name="acc", bufs=6)
+            acc = psum.tile([P, H], F32, name="acc", bufs=7)
             for a in range(PASSES):
                 nc.tensor.matmul_mx(
                     out=acc[:],
@@ -146,49 +145,30 @@ def tile_list_hboth_silu_kernel(tc, xT, w, wgt, b, wgo, offs, offs2, out):
         def store(m):
             nc.sync.dma_start(out=out[m * P : (m + 1) * P, :], in_=window[m][:])
 
-        for i in range(PACK):
-            for h in range(HALVES):
-                gather(0, i, h)
-        for h in range(HALVES):
-            interleave_x(0, h)
-        for i in range(PACK):
-            for h in range(HALVES):
-                gather(1, i, h)
-            if i >= 2:
-                quantize_x(0, i - 2)
-        for h in range(HALVES):
-            interleave_x(1, h)
         for a in range(PASSES):
-            interleave_w(0, a, nc.vector.tensor_copy)
+            for i in range(PACK):
+                for h in range(HALVES):
+                    gather(a, i, h)
+            for h in range(HALVES):
+                interleave_x(a, h)
+        interleave_w(0, 0, nc.scalar.copy)
+        interleave_w(0, 1, nc.vector.tensor_copy)
+        quantize_x(0, 0)
         quantize_x(1, 0)
         quantize_w(0)
         product(0, 0)
+        quantize_x(0, 1)
         quantize_x(1, 1)
         product(0, 1)
-        for a in range(PASSES):
-            interleave_w(1, a, nc.scalar.copy)
-        scatter(0, 0)
-        quantize_w(1)
-        product(1, 0)
-        for a in range(PASSES):
-            interleave_w(2, a, nc.scalar.copy)
-        scatter(0, 1)
-        store(0)
-        quantize_w(2)
-        product(2, 0)
-        product(1, 1)
-        scatter(1, 0)
-        for a in range(PASSES):
-            interleave_w(3, a, nc.scalar.copy)
-        scatter(2, 0)
-        quantize_w(3)
-        product(3, 0)
-        scatter(1, 1)
-        store(1)
-        product(2, 1)
-        scatter(3, 0)
-        product(3, 1)
-        scatter(2, 1)
-        store(2)
-        scatter(3, 1)
-        store(3)
+        for m, copies in ((1, (nc.scalar.copy, nc.vector.tensor_copy)), (2, (nc.scalar.copy, nc.scalar.copy)), (3, (nc.vector.tensor_copy, nc.vector.tensor_copy))):
+            for a in range(PASSES):
+                interleave_w(m, a, copies[a])
+            quantize_w(m)
+            for h in range(HALVES):
+                product(m, h)
+        for m in (0, 2):
+            for h in range(HALVES):
+                for mm in (m, m + 1):
+                    scatter(mm, h)
+                    if h == 1:
+                        store(mm)

@@ -38,7 +38,7 @@ def tile_list_hboth_silu_kernel(tc, xT, w, wgt, b, wgo, offs, offs2, out):
         offs2_sb = lists.tile([P, S // 16], U16, name="offs2_sb")
 
         wgt_sb = [keep.tile([P, H], F32, name=f"wgt{h}") for h in range(HALVES)]
-        wgo_sb = keep.tile([P, S], F32, name="wgo_sb")
+        wgo_sb = [keep.tile([P, H], F32, name=f"wgo{h}") for h in range(HALVES)]
         x_sb = [[keep.tile([P, T], F32, name=f"x{a}{i}") for i in range(PACK)] for a in range(PASSES)]
         w_raw0 = keep.tile([P, PACK, M], F32, name="w_raw0")
         w_raw1 = [keep.tile([P, PACK, 2 * P], F32, name=f"w_raw1{g}") for g in range(2)]
@@ -75,7 +75,8 @@ def tile_list_hboth_silu_kernel(tc, xT, w, wgt, b, wgo, offs, offs2, out):
         for g in range(2):
             nc.sync.dma_start(out=w_raw1[g][:], in_=w_hbm[1, :, :, 2 * P * g : 2 * P * (g + 1)])
         nc.sync.dma_start(offs2_sb[:], offs2)
-        nc.sync.dma_start(out=wgo_sb[:], in_=wgo)
+        for h in range(HALVES):
+            nc.sync.dma_start(out=wgo_sb[h][:], in_=wgo[:, h * H : (h + 1) * H])
 
         make_identity(nc, ident[:])
         for m in range(MT):
@@ -138,12 +139,17 @@ def tile_list_hboth_silu_kernel(tc, xT, w, wgt, b, wgo, offs, offs2, out):
             nc.vector.tensor_tensor(
                 window[m][:].indirect(offs2_sb[:, h * HC : (h + 1) * HC]),
                 act[m][h][:],
-                wgo_sb[:, h * H : (h + 1) * H],
+                wgo_sb[h][:],
                 MULT,
             )
 
         def store(m):
-            nc.sync.dma_start(out=out[m * P : (m + 1) * P, :], in_=window[m][:])
+            rows = slice(m * P, (m + 1) * P)
+            if m < MT - 1:
+                nc.sync.dma_start(out=out[rows, :], in_=window[m][:])
+            else:
+                nc.sync.dma_start(out=out[rows, 0 : T // 2], in_=window[m][:, 0 : T // 2])
+                nc.scalar.dma_start(out=out[rows, T // 2 : T], in_=window[m][:, T // 2 : T])
 
         for a in range(PASSES):
             for i in range(PACK):
@@ -164,7 +170,11 @@ def tile_list_hboth_silu_kernel(tc, xT, w, wgt, b, wgo, offs, offs2, out):
             for a in range(PASSES):
                 interleave_w(m, a, copies[a])
             quantize_w(m)
-            for h in range(HALVES):
+            if m == 1:
+                product(1, 0)
+                product(1, 1)
+        for h in range(HALVES):
+            for m in (2, 3):
                 product(m, h)
         for m in (0, 2):
             for h in range(HALVES):

@@ -43,9 +43,10 @@ def tile_list_hboth_silu_kernel(tc, xT, w, wgt, b, wgo, offs, offs2, out):
         w_raw0 = keep.tile([P, PACK, M], F32, name="w_raw0")
         w_raw1 = [keep.tile([P, PACK, 2 * P], F32, name=f"w_raw1{g}") for g in range(2)]
         picked = [[keep.tile([P, PACK, H], F32, name=f"g{a}{h}") for h in range(HALVES)] for a in range(PASSES)]
-        x_bf = [[keep.tile([P, H, PACK], BF16, align_bytes=64, name=f"xb{a}{h}") for h in range(HALVES)] for a in range(PASSES)]
-        x_codes = [[keep.tile([P, H], U32, align_bytes=64, name=f"xc{a}{h}") for h in range(HALVES)] for a in range(PASSES)]
-        x_scales = [[keep.tile([P, H], U8, align_bytes=64, name=f"xs{a}{h}") for h in range(HALVES)] for a in range(PASSES)]
+        x_width = ((S,), (H, H))
+        x_bf = [[keep.tile([P, n, PACK], BF16, align_bytes=64, name=f"xb{a}{k}") for k, n in enumerate(x_width[a])] for a in range(PASSES)]
+        x_codes = [[keep.tile([P, n], U32, align_bytes=64, name=f"xc{a}{k}") for k, n in enumerate(x_width[a])] for a in range(PASSES)]
+        x_scales = [[keep.tile([P, n], U8, align_bytes=64, name=f"xs{a}{k}") for k, n in enumerate(x_width[a])] for a in range(PASSES)]
         w_bf = [keep.tile([P, PASSES * P, PACK], BF16, align_bytes=64, name=f"wb{m}") for m in range(MT)]
         w_codes = [keep.tile([P, PASSES * P], U32, align_bytes=64, name=f"wc{m}") for m in range(MT)]
         w_scales = [keep.tile([P, PASSES * P], U8, align_bytes=64, name=f"ws{m}") for m in range(MT)]
@@ -80,7 +81,7 @@ def tile_list_hboth_silu_kernel(tc, xT, w, wgt, b, wgo, offs, offs2, out):
 
         make_identity(nc, ident[:])
         for m in range(MT):
-            (nc.vector if m < 2 else nc.gpsimd).memset(window[m][:], 0.0)
+            (nc.vector if m < 3 else nc.gpsimd).memset(window[m][:], 0.0)
         nc.scalar.dma_start(out=b_rows[0:MT, :], in_=b.rearrange("(m p) -> m p", p=P))
         b_ps = psum.tile([P, P], F32, name="b_ps")
         nc.tensor.transpose(b_ps[:], b_rows[:], ident[:])
@@ -94,9 +95,12 @@ def tile_list_hboth_silu_kernel(tc, xT, w, wgt, b, wgo, offs, offs2, out):
                 MULT,
             )
 
+        def x_part(tiles, a, h):
+            return tiles[0][0][:, h * H : (h + 1) * H] if a == 0 else tiles[1][h][:]
+
         def interleave_x(a, h):
             nc.scalar.copy(
-                out=x_bf[a][h][:].rearrange("p (c e) i -> p c i e", e=4),
+                out=x_part(x_bf, a, h).rearrange("p (c e) i -> p c i e", e=4),
                 in_=picked[a][h][:].rearrange("p i (c e) -> p c i e", e=4),
             )
 
@@ -128,8 +132,8 @@ def tile_list_hboth_silu_kernel(tc, xT, w, wgt, b, wgo, offs, offs2, out):
                     out=acc[:],
                     lhsT=w_codes[m][:, a * P : (a + 1) * P].bitcast(FP8X4),
                     lhsT_scale=w_scales[m][:, a * P : (a + 1) * P],
-                    rhs=x_codes[a][h][:].bitcast(FP8X4),
-                    rhs_scale=x_scales[a][h][:],
+                    rhs=x_part(x_codes, a, h).bitcast(FP8X4),
+                    rhs_scale=x_part(x_scales, a, h),
                     start=(a == 0),
                     stop=(a == PASSES - 1),
                 )
@@ -163,7 +167,6 @@ def tile_list_hboth_silu_kernel(tc, xT, w, wgt, b, wgo, offs, offs2, out):
         quantize_x(1, 0)
         quantize_w(0)
         product(0, 0)
-        quantize_x(0, 1)
         quantize_x(1, 1)
         product(0, 1)
         for m, copies in ((1, (nc.scalar.copy, nc.vector.tensor_copy)), (2, (nc.scalar.copy, nc.scalar.copy)), (3, (nc.vector.tensor_copy, nc.vector.tensor_copy))):

from contextlib import ExitStack

import concourse.mybir as mybir
from concourse.masks import make_identity

K, M, T, S = 1024, 512, 1024, 512
FLOPS = 2 * K * M * S

F32 = mybir.dt.float32
BF16 = mybir.dt.bfloat16
U32 = mybir.dt.uint32
U16 = mybir.dt.uint16
U8 = mybir.dt.uint8
FP8X4 = mybir.dt.float8_e4m3fn_x4
MULT = mybir.AluOpType.mult
SILU = mybir.ActivationFunctionType.Silu

P = 128
PACK = 4
PASSES = K // (P * PACK)
MT = M // P
HALVES = 2
H = S // HALVES
HC = H // 16


def tile_list_hboth_silu_kernel(tc, xT, w, wgt, b, wgo, offs, offs2, out):
    nc = tc.nc
    x_hbm = xT.rearrange("(a p i) t -> a p i t", p=P, i=PACK)
    w_hbm = w.rearrange("(a p i) n -> a p i n", p=P, i=PACK)

    with ExitStack() as ctx:
        lists = ctx.enter_context(tc.tile_pool(name="lists", bufs=1))
        keep = ctx.enter_context(tc.tile_pool(name="keep", bufs=1))
        psum = ctx.enter_context(tc.psum_pool(name="psum", bufs=1))

        offs_sb = lists.tile([P, S // 16], U16, name="offs_sb")
        offs2_sb = lists.tile([P, S // 16], U16, name="offs2_sb")

        wgt_sb = [keep.tile([P, H], F32, name=f"wgt{h}") for h in range(HALVES)]
        wgo_sb = [keep.tile([P, H], F32, name=f"wgo{h}") for h in range(HALVES)]
        x_sb = [[keep.tile([P, T], F32, name=f"x{a}{i}") for i in range(PACK)] for a in range(PASSES)]
        w_raw0 = keep.tile([P, PACK, M], F32, name="w_raw0")
        w_raw1 = [keep.tile([P, PACK, 2 * P], F32, name=f"w_raw1{g}") for g in range(2)]
        picked = [[keep.tile([P, PACK, H], F32, name=f"g{a}{h}") for h in range(HALVES)] for a in range(PASSES)]
        x_width = ((S,), (H, H))
        x_bf = [[keep.tile([P, n, PACK], BF16, align_bytes=64, name=f"xb{a}{k}") for k, n in enumerate(x_width[a])] for a in range(PASSES)]
        x_codes = [[keep.tile([P, n], U32, align_bytes=64, name=f"xc{a}{k}") for k, n in enumerate(x_width[a])] for a in range(PASSES)]
        x_scales = [[keep.tile([P, n], U8, align_bytes=64, name=f"xs{a}{k}") for k, n in enumerate(x_width[a])] for a in range(PASSES)]
        w_bf = [keep.tile([P, PASSES * P, PACK], BF16, align_bytes=64, name=f"wb{m}") for m in range(MT)]
        w_codes = [keep.tile([P, PASSES * P], U32, align_bytes=64, name=f"wc{m}") for m in range(MT)]
        w_scales = [keep.tile([P, PASSES * P], U8, align_bytes=64, name=f"ws{m}") for m in range(MT)]
        window = [keep.tile([P, T], F32, name=f"win{m}") for m in range(MT)]
        act = [[keep.tile([P, H], F32, name=f"act{m}{h}") for h in range(HALVES)] for m in range(MT)]

        ident = keep.tile([P, P], F32, name="ident")
        b_rows = keep.tile([P, P], F32, name="b_rows")
        b_cols = keep.tile([P, MT], F32, name="b_cols")
        warm_in = keep.tile([P, 1], F32, name="warm_in")
        warm_out = keep.tile([P, 1], F32, name="warm_out")

        nc.vector.memset(warm_in[:], 0.0)
        nc.vector.memset(b_rows[:], 0.0)
        nc.sync.dma_start(offs_sb[:], offs)
        nc.sync.dma_start(out=x_sb[0][0][:], in_=x_hbm[0, :, 0, :])
        nc.sync.dma_start(out=wgt_sb[0][:], in_=wgt[:, 0:H])
        nc.sync.dma_start(out=wgt_sb[1][:], in_=wgt[:, H:S])
        nc.scalar.activation(warm_out[:], warm_in[:], SILU)
        def load_x(a, i):
            nc.sync.dma_start(out=x_sb[a][i][:], in_=x_hbm[a, :, i, :])

        for a, i in ((0, 1), (0, 2), (0, 3), (1, 0), (1, 1), (1, 2)):
            load_x(a, i)
        nc.sync.dma_start(out=w_raw0[:], in_=w_hbm[0])
        load_x(1, 3)
        for g in range(2):
            nc.sync.dma_start(out=w_raw1[g][:], in_=w_hbm[1, :, :, 2 * P * g : 2 * P * (g + 1)])
        nc.sync.dma_start(offs2_sb[:], offs2)
        for h in range(HALVES):
            nc.sync.dma_start(out=wgo_sb[h][:], in_=wgo[:, h * H : (h + 1) * H])

        make_identity(nc, ident[:])
        for m in range(MT):
            (nc.vector if m < 3 else nc.gpsimd).memset(window[m][:], 0.0)
        nc.scalar.dma_start(out=b_rows[0:MT, :], in_=b.rearrange("(m p) -> m p", p=P))
        b_ps = psum.tile([P, P], F32, name="b_ps")
        nc.tensor.transpose(b_ps[:], b_rows[:], ident[:])
        nc.scalar.copy(out=b_cols[:], in_=b_ps[:, 0:MT])

        def gather(a, i, h):
            nc.vector.tensor_tensor(
                picked[a][h][:, i, :],
                x_sb[a][i][:].indirect(offs_sb[:, h * HC : (h + 1) * HC]),
                wgt_sb[h][:],
                MULT,
            )

        def x_part(tiles, a, h):
            return tiles[0][0][:, h * H : (h + 1) * H] if a == 0 else tiles[1][h][:]

        def interleave_x(a, h):
            nc.scalar.copy(
                out=x_part(x_bf, a, h).rearrange("p (c e) i -> p c i e", e=4),
                in_=picked[a][h][:].rearrange("p i (c e) -> p c i e", e=4),
            )

        def quantize_x(a, h):
            nc.vector.quantize_mx(
                out=x_codes[a][h][:].bitcast(FP8X4),
                scales=x_scales[a][h][:],
                in_=x_bf[a][h][:].rearrange("p c i -> p (c i)"),
            )

        def interleave_w(m, a, copy):
            raw = w_raw0[:, :, m * P : (m + 1) * P] if a == 0 else w_raw1[m // 2][:, :, (m % 2) * P : (m % 2 + 1) * P]
            copy(
                out=w_bf[m][:, a * P : (a + 1) * P, :].rearrange("p (c e) i -> p c i e", e=4),
                in_=raw.rearrange("p i (c e) -> p c i e", e=4),
            )

        def quantize_w(m):
            nc.vector.quantize_mx(
                out=w_codes[m][:].bitcast(FP8X4),
                scales=w_scales[m][:],
                in_=w_bf[m][:].rearrange("p c i -> p (c i)"),
            )

        def product(m, h):
            acc = psum.tile([P, H], F32, name="acc", bufs=7)
            for a in range(PASSES):
                nc.tensor.matmul_mx(
                    out=acc[:],
                    lhsT=w_codes[m][:, a * P : (a + 1) * P].bitcast(FP8X4),
                    lhsT_scale=w_scales[m][:, a * P : (a + 1) * P],
                    rhs=x_part(x_codes, a, h).bitcast(FP8X4),
                    rhs_scale=x_part(x_scales, a, h),
                    start=(a == 0),
                    stop=(a == PASSES - 1),
                )
            nc.scalar.activation(act[m][h][:], acc[:], SILU, bias=b_cols[:, m : m + 1])

        def scatter(m, h):
            nc.vector.tensor_tensor(
                window[m][:].indirect(offs2_sb[:, h * HC : (h + 1) * HC]),
                act[m][h][:],
                wgo_sb[h][:],
                MULT,
            )

        def store(m):
            rows = slice(m * P, (m + 1) * P)
            if m < MT - 1:
                nc.sync.dma_start(out=out[rows, :], in_=window[m][:])
            else:
                nc.sync.dma_start(out=out[rows, 0 : T // 2], in_=window[m][:, 0 : T // 2])
                nc.scalar.dma_start(out=out[rows, T // 2 : T], in_=window[m][:, T // 2 : T])

        for a in range(PASSES):
            for i in range(PACK):
                for h in range(HALVES):
                    gather(a, i, h)
            for h in range(HALVES):
                interleave_x(a, h)
        interleave_w(0, 0, nc.scalar.copy)
        interleave_w(0, 1, nc.vector.tensor_copy)
        quantize_x(0, 0)
        quantize_x(1, 0)
        quantize_w(0)
        product(0, 0)
        quantize_x(1, 1)
        product(0, 1)
        for m, copies in ((1, (nc.scalar.copy, nc.vector.tensor_copy)), (2, (nc.scalar.copy, nc.scalar.copy)), (3, (nc.vector.tensor_copy, nc.vector.tensor_copy))):
            for a in range(PASSES):
                interleave_w(m, a, copies[a])
            quantize_w(m)
            if m == 1:
                product(1, 0)
                product(1, 1)
        for h in range(HALVES):
            for m in (2, 3):
                product(m, h)
        for m in (0, 2):
            for h in range(HALVES):
                for mm in (m, m + 1):
                    scatter(mm, h)
                    if h == 1:
                        store(mm)
